import numpy as np
import ml_dtypes


def mxq(x, axis, fmt="e4m3"):
    dtype, down = {"e4m3": (ml_dtypes.float8_e4m3fn, 7), "e5m2": (ml_dtypes.float8_e5m2, 14)}[fmt]
    v = np.moveaxis(np.asarray(x, np.float32).astype(ml_dtypes.bfloat16).astype(np.float64), axis, -1)
    blocks = v.reshape(v.shape[:-1] + (-1, 32))
    amax = np.abs(blocks).max(-1, keepdims=True)
    byte = np.maximum(np.where(amax > 0, np.frexp(amax)[1] - 1 + 127, 0) - down, 1)
    scale = np.exp2(byte - 127.0)
    codes = (blocks / scale).astype(np.float32).astype(dtype).astype(np.float64)
    return np.moveaxis((codes * scale).reshape(v.shape), -1, axis)


WIDE = False


def mx_kscale(k):
    if not WIDE:
        return np.ones(k)
    levels = np.array([10, -10, 5, -5, 0])
    if k % 512:
        return np.exp2(np.random.permutation(np.resize(levels, k // 32))).repeat(32)
    a = np.empty((k // 512, 16))
    for p in range(k // 512):
        a[p, :8] = np.random.permutation(np.resize(levels, 8))
        for g in range(8):
            far = levels[np.abs(levels - a[p, g]) >= 10]
            a[p, g + 8] = far[np.random.randint(len(far))]
    return np.exp2(a.ravel()).repeat(32)


def f64(x):
    return np.asarray(x).astype(np.float64)


def striped8(idx):
    return np.concatenate([v.reshape(-1, 16).T for v in idx]).astype(np.uint16)


def unstriped8(offs):
    return np.stack([offs[16 * g:16 * g + 16].T.reshape(-1) for g in range(8)]).astype(np.int64)


E2M1 = np.array([0.0, 0.5, 1.0, 1.5, 2.0, 3.0, 4.0, 6.0, -0.0, -0.5, -1.0, -1.5, -2.0, -3.0, -4.0, -6.0])


def pack_weight(w, fmt):
    k, n = w.shape
    w = f64(np.asarray(w, np.float32).astype(ml_dtypes.bfloat16)).reshape(k // 32, 32, n)
    amax = np.abs(w).max(1)
    if fmt == "e4m3":
        byte = np.frexp(amax)[1] - 1 + 127 - 7
    else:
        mant, ex = np.frexp(amax / 6.0)
        byte = np.where(mant > 0.5, ex, ex - 1) + 127
    byte = np.clip(np.where(amax > 0, byte, 1), 1, 254)
    scaled = (w * np.exp2(127.0 - byte)[:, None, :]).reshape(k, n).astype(np.float32)
    by_word = np.ascontiguousarray(scaled.reshape(k // 512, 128, 4, n).transpose(0, 1, 3, 2))
    if fmt == "e4m3":
        words = by_word.astype(ml_dtypes.float8_e4m3fn).view(np.uint8)
    else:
        c = by_word.astype(ml_dtypes.float4_e2m1fn).view(np.uint8) & 0xF
        words = (c[..., 0::2] | (c[..., 1::2] << 4)).reshape(k // 512, 128, 2 * n)
    return np.ascontiguousarray(words), np.ascontiguousarray(byte.astype(np.uint8).reshape(k // 512, 16, n))


def unpack_weight(words, scales, fmt):
    g, _, n = scales.shape
    words = np.ascontiguousarray(words).reshape(g, 128, n, -1)
    if fmt == "e4m3":
        vals = words.view(ml_dtypes.float8_e4m3fn).astype(np.float64)
    else:
        nib = np.empty((g, 128, n, 4), np.uint8)
        nib[..., 0::2] = words & 0xF
        nib[..., 1::2] = words >> 4
        vals = E2M1[nib]
    vals = vals * np.repeat(np.exp2(scales.astype(np.float64) - 127.0), 8, axis=1)[..., None]
    return vals.transpose(0, 1, 3, 2).reshape(g * 512, n)


def silu(v):
    return v / (1.0 + np.exp(-np.maximum(v, -700.0)))


K, M, T, S = 2048, 256, 1024, 512


def setup_inputs():
    n = np.random.standard_normal
    s = mx_kscale(K)[:, None]
    p_w = pack_weight(n((K, M)) / np.sqrt(K) / s, "e2m1")
    return {
        "xT": (n((K, T)) * s).astype(np.float32),
        "w_words": p_w[0],
        "w_scales": p_w[1],
        "wgt": np.repeat(np.random.uniform(0.5, 2.0, (8, S)), 16, axis=0).astype(np.float32),
        "b": (0.3 * n(256)).astype(np.float32),
        "offs": striped8(np.stack([np.random.permutation(T)[:S] for _ in range(8)])),
    }


def reference(xT, w_words, w_scales, wgt, b, offs):
    idx = unstriped8(offs)
    group = np.arange(K) % 512 // 64
    xg = f64(wgt)[np.arange(K) // 4 % 128] * f64(xT)[np.arange(K)[:, None], idx[group]]
    xT_ = mxq(xg, 0, "e4m3")
    w_ = unpack_weight(w_words, w_scales, "e2m1")
    y = w_.T @ xT_
    return silu(y + f64(b)[:, None])

@@ -1,0 +1,144 @@
+import concourse.mybir as mybir
+
+K, M, T, S = 2048, 256, 1024, 512
+FLOPS = 2 * K * M * S
+
+P = 128
+PACK = 4
+PASSES = K // (P * PACK)
+BLOCK = 128
+
+F32 = mybir.dt.float32
+BF16 = mybir.dt.bfloat16
+I32 = mybir.dt.int32
+U32 = mybir.dt.uint32
+U16 = mybir.dt.uint16
+U8 = mybir.dt.uint8
+FP8X4 = mybir.dt.float8_e4m3fn_x4
+FP4X4 = mybir.dt.float4_e2m1fn_x4
+MULT = mybir.AluOpType.mult
+SILU = mybir.ActivationFunctionType.Silu
+
+
+def tile_list_heads_silu_kernel(tc, xT, w_words, w_scales, wgt, b, offs, out):
+    nc = tc.nc
+    with tc.tile_pool(name="held", bufs=1) as held, tc.psum_pool(name="psum", bufs=1) as psum:
+        lists = held.tile([P, S // 16], U16, name="lists")
+        factors = held.tile([P, S], F32, name="factors")
+        planes = [held.tile([P, T], F32, name=f"plane{u}") for u in range(PASSES * PACK)]
+        words = held.tile([P, PASSES, 2 * M], U8, name="words", align_bytes=64)
+        wscales = held.tile([P, PASSES, M], U8, name="wscales", align_bytes=64)
+        bias = held.tile([P, 2], F32, name="bias")
+        warm = held.tile([P, 1], F32, name="warm")
+        picked = [held.tile([P, PACK, S], F32, name=f"picked{g}") for g in range(PASSES)]
+        packed = [held.tile([P, S, PACK], BF16, name=f"packed{g}", align_bytes=64) for g in range(PASSES)]
+        codes = [held.tile([P, S], U32, name=f"codes{g}", align_bytes=64) for g in range(PASSES)]
+        scales = [held.tile([P, S], U8, name=f"scales{g}", align_bytes=64) for g in range(PASSES)]
+        result = [held.tile([P, S], F32, name=f"result{m}") for m in range(2)]
+        sums = [[psum.tile([P, BLOCK], F32, name=f"sum{m}_{j}") for j in range(S // BLOCK)] for m in range(2)]
+
+        nc.vector.memset(warm[:], 0.0)
+        nc.vector.memset(wscales[:].rearrange("p a n -> p (a n)").bitcast(I32), 0)
+        nc.scalar.activation(warm[:], warm[:], SILU)
+
+        x_planes = xT.rearrange("(a p i) t -> a i p t", p=P, i=PACK)
+        scale_rows = w_scales.bitcast(I32).rearrange("a (q r) n -> r q a n", r=4)
+
+        def load_plane(u):
+            nc.sync.dma_start(out=planes[u][:], in_=x_planes[u // PACK, u % PACK])
+
+        nc.sync.dma_start(lists[:], offs)
+        nc.sync.dma_start(out=factors[:, 0:256], in_=wgt[:, 0:256])
+        load_plane(0)
+        nc.sync.dma_start(out=factors[:, 256:512], in_=wgt[:, 256:512])
+        for u in range(1, 10):
+            load_plane(u)
+        nc.sync.dma_start(out=words[:].bitcast(I32), in_=w_words.bitcast(I32).rearrange("a p n -> p a n"))
+        for r in range(4):
+            nc.sync.dma_start(out=wscales[r:P:32, :, :].bitcast(I32), in_=scale_rows[r])
+        load_plane(10)
+        nc.sync.dma_start(out=bias[:], in_=b.rearrange("(c p) -> p c", p=P))
+        for u in range(11, 16):
+            load_plane(u)
+
+        def gather(g, t, lo, hi):
+            nc.vector.tensor_tensor(
+                picked[g][:, t, lo:hi], planes[PACK * g + t][:].indirect(lists[:, lo // 16 : hi // 16]), factors[:, lo:hi], MULT
+            )
+
+        def interleave(g, lo, hi, vector=False):
+            src = picked[g][:, :, lo:hi].rearrange("p t n -> p n t")
+            if vector:
+                nc.vector.tensor_copy(packed[g][:, lo:hi, :], src)
+            else:
+                nc.scalar.copy(packed[g][:, lo:hi, :], src)
+
+        def quantize(g, lo, hi):
+            nc.vector.quantize_mx(
+                out=codes[g][:, lo:hi].bitcast(FP8X4),
+                scales=scales[g][:, lo:hi],
+                in_=packed[g][:, lo:hi, :].rearrange("p n t -> p (n t)"),
+            )
+
+        def multiply(g, lo, hi):
+            for j in range(lo // BLOCK, hi // BLOCK):
+                cols = slice(BLOCK * j, BLOCK * (j + 1))
+                for m in range(2):
+                    nc.tensor.matmul_mx(
+                        out=sums[m][j][:],
+                        lhsT=words[:, g, 256 * m : 256 * (m + 1)].bitcast(FP4X4),
+                        lhsT_scale=wscales[:, g, P * m : P * (m + 1)],
+                        rhs=codes[g][:, cols].bitcast(FP8X4),
+                        rhs_scale=scales[g][:, cols],
+                        start=(g == 0),
+                        stop=(g == PASSES - 1),
+                    )
+
+        def finish(lo, hi):
+            for m in range(2):
+                for j in range(lo // BLOCK, hi // BLOCK):
+                    nc.scalar.activation(result[m][:, BLOCK * j : BLOCK * (j + 1)], sums[m][j][:], SILU, bias=bias[:, m : m + 1])
+                nc.sync.dma_start(out=out[P * m : P * (m + 1), lo:hi], in_=result[m][:, lo:hi])
+
+        for t in range(4):
+            gather(0, t, 0, 256)
+            gather(0, t, 256, 512)
+        interleave(0, 0, 256)
+        interleave(0, 256, 512)
+        for t in range(4):
+            gather(1, t, 0, 256)
+            gather(1, t, 256, 512)
+            if t == 2:
+                quantize(0, 0, 512)
+                multiply(0, 0, 512)
+        interleave(1, 0, 256)
+        interleave(1, 256, 512)
+        for t in range(4):
+            gather(2, t, 0, 384)
+        interleave(2, 0, 384)
+        quantize(1, 0, 512)
+        multiply(1, 0, 512)
+        for t in range(4):
+            gather(3, t, 0, 384)
+        quantize(2, 0, 256)
+        quantize(2, 256, 384)
+        multiply(2, 0, 384)
+        interleave(3, 0, 256)
+        interleave(3, 256, 384)
+        for t in range(4):
+            gather(2, t, 384, 512)
+        interleave(2, 384, 512)
+        quantize(3, 0, 256)
+        multiply(3, 0, 256)
+        for t in range(4):
+            gather(3, t, 384, 512)
+            if t == 1:
+                quantize(3, 256, 384)
+                multiply(3, 256, 384)
+        interleave(3, 384, 512, vector=True)
+        finish(0, 384)
+        quantize(2, 384, 512)
+        multiply(2, 384, 512)
+        quantize(3, 384, 512)
+        multiply(3, 384, 512)
+        finish(384, 512)

@@ -37,9 +37,8 @@ def tile_list_heads_silu_kernel(tc, xT, w_words, w_scales, wgt, b, offs, out):
         result = [held.tile([P, S], F32, name=f"result{m}") for m in range(2)]
         sums = [[psum.tile([P, BLOCK], F32, name=f"sum{m}_{j}") for j in range(S // BLOCK)] for m in range(2)]
 
-        nc.vector.memset(warm[:], 0.0)
         nc.vector.memset(wscales[:].rearrange("p a n -> p (a n)").bitcast(I32), 0)
-        nc.scalar.activation(warm[:], warm[:], SILU)
+        nc.vector.memset(warm[:], 0.0)
 
         x_planes = xT.rearrange("(a p i) t -> a i p t", p=P, i=PACK)
         scale_rows = w_scales.bitcast(I32).rearrange("a (q r) n -> r q a n", r=4)
@@ -48,18 +47,18 @@ def tile_list_heads_silu_kernel(tc, xT, w_words, w_scales, wgt, b, offs, out):
             nc.sync.dma_start(out=planes[u][:], in_=x_planes[u // PACK, u % PACK])
 
         nc.sync.dma_start(lists[:], offs)
-        nc.sync.dma_start(out=factors[:, 0:256], in_=wgt[:, 0:256])
+        nc.scalar.dma_start(out=factors[:, 0:256], in_=wgt[:, 0:256])
         load_plane(0)
+        for r in range(4):
+            nc.scalar.dma_start(out=wscales[r:P:32, :, :].bitcast(I32), in_=scale_rows[r])
+        nc.scalar.activation(warm[:], warm[:], SILU)
         nc.sync.dma_start(out=factors[:, 256:512], in_=wgt[:, 256:512])
         for u in range(1, 10):
             load_plane(u)
         nc.sync.dma_start(out=words[:].bitcast(I32), in_=w_words.bitcast(I32).rearrange("a p n -> p a n"))
-        for r in range(4):
-            nc.sync.dma_start(out=wscales[r:P:32, :, :].bitcast(I32), in_=scale_rows[r])
-        load_plane(10)
-        nc.sync.dma_start(out=bias[:], in_=b.rearrange("(c p) -> p c", p=P))
-        for u in range(11, 16):
+        for u in range(10, 16):
             load_plane(u)
+        nc.sync.dma_start(out=bias[:], in_=b.rearrange("(c p) -> p c", p=P))
 
         def gather(g, t, lo, hi):
             nc.vector.tensor_tensor(
@@ -115,30 +114,37 @@ def tile_list_heads_silu_kernel(tc, xT, w_words, w_scales, wgt, b, offs, out):
         interleave(1, 256, 512)
         for t in range(4):
             gather(2, t, 0, 384)
-        interleave(2, 0, 384)
-        quantize(1, 0, 512)
-        multiply(1, 0, 512)
-        for t in range(4):
-            gather(3, t, 0, 384)
+            if t == 2:
+                quantize(1, 0, 512)
+                multiply(1, 0, 512)
+        interleave(2, 0, 256)
+        interleave(2, 256, 384)
+        gather(3, 0, 0, 384)
+        gather(3, 1, 0, 384)
+        gather(2, 0, 384, 512)
+        gather(2, 1, 384, 512)
+        gather(2, 2, 384, 512)
+        gather(2, 3, 384, 512)
+        interleave(2, 384, 512)
+        gather(3, 2, 0, 384)
         quantize(2, 0, 256)
         quantize(2, 256, 384)
         multiply(2, 0, 384)
+        gather(3, 3, 0, 384)
         interleave(3, 0, 256)
-        interleave(3, 256, 384)
-        for t in range(4):
-            gather(2, t, 384, 512)
-        interleave(2, 384, 512)
-        quantize(3, 0, 256)
-        multiply(3, 0, 256)
-        for t in range(4):
-            gather(3, t, 384, 512)
-            if t == 1:
-                quantize(3, 256, 384)
-                multiply(3, 256, 384)
-        interleave(3, 384, 512, vector=True)
-        finish(0, 384)
         quantize(2, 384, 512)
         multiply(2, 384, 512)
+        gather(3, 0, 384, 512)
+        interleave(3, 256, 384, vector=True)
+        gather(3, 1, 384, 512)
+        gather(3, 2, 384, 512)
+        gather(3, 3, 384, 512)
+        quantize(3, 0, 256)
+        multiply(3, 0, 256)
+        interleave(3, 384, 512, vector=True)
+        quantize(3, 256, 384)
+        multiply(3, 256, 384)
+        finish(0, 384)
         quantize(3, 384, 512)
         multiply(3, 384, 512)
         finish(384, 512)

@@ -65,12 +65,12 @@ def tile_list_heads_silu_kernel(tc, xT, w_words, w_scales, wgt, b, offs, out):
                 picked[g][:, t, lo:hi], planes[PACK * g + t][:].indirect(lists[:, lo // 16 : hi // 16]), factors[:, lo:hi], MULT
             )
 
-        def interleave(g, lo, hi, vector=False):
-            src = picked[g][:, :, lo:hi].rearrange("p t n -> p n t")
+        def interleave(g, t0, t1, lo, hi, vector=False):
+            src = picked[g][:, t0:t1, lo:hi].rearrange("p t n -> p n t")
             if vector:
-                nc.vector.tensor_copy(packed[g][:, lo:hi, :], src)
+                nc.vector.tensor_copy(packed[g][:, lo:hi, t0:t1], src)
             else:
-                nc.scalar.copy(packed[g][:, lo:hi, :], src)
+                nc.scalar.copy(packed[g][:, lo:hi, t0:t1], src)
 
         def quantize(g, lo, hi):
             nc.vector.quantize_mx(
@@ -99,52 +99,27 @@ def tile_list_heads_silu_kernel(tc, xT, w_words, w_scales, wgt, b, offs, out):
                     nc.scalar.activation(result[m][:, BLOCK * j : BLOCK * (j + 1)], sums[m][j][:], SILU, bias=bias[:, m : m + 1])
                 nc.sync.dma_start(out=out[P * m : P * (m + 1), lo:hi], in_=result[m][:, lo:hi])
 
-        for t in range(4):
-            gather(0, t, 0, 256)
-            gather(0, t, 256, 512)
-        interleave(0, 0, 256)
-        interleave(0, 256, 512)
-        for t in range(4):
-            gather(1, t, 0, 256)
-            gather(1, t, 256, 512)
-            if t == 2:
-                quantize(0, 0, 512)
-                multiply(0, 0, 512)
-        interleave(1, 0, 256)
-        interleave(1, 256, 512)
-        for t in range(4):
-            gather(2, t, 0, 384)
-            if t == 2:
-                quantize(1, 0, 512)
-                multiply(1, 0, 512)
-        interleave(2, 0, 256)
-        interleave(2, 256, 384)
-        gather(3, 0, 0, 384)
-        gather(3, 1, 0, 384)
-        gather(2, 0, 384, 512)
-        gather(2, 1, 384, 512)
-        gather(2, 2, 384, 512)
-        gather(2, 3, 384, 512)
-        interleave(2, 384, 512)
-        gather(3, 2, 0, 384)
-        quantize(2, 0, 256)
-        quantize(2, 256, 384)
-        multiply(2, 0, 384)
-        gather(3, 3, 0, 384)
-        interleave(3, 0, 256)
-        quantize(2, 384, 512)
-        multiply(2, 384, 512)
-        gather(3, 0, 384, 512)
-        interleave(3, 256, 384, vector=True)
-        gather(3, 1, 384, 512)
-        gather(3, 2, 384, 512)
-        gather(3, 3, 384, 512)
+        for g in range(PASSES):
+            for t in range(PACK):
+                gather(g, t, 0, 256)
+                gather(g, t, 256, 512)
+                if t == 1 and g >= 2:
+                    interleave(g, 0, 2, 0, 256)
+                    interleave(g, 0, 2, 256, 512)
+                if t == 2 and g >= 1:
+                    quantize(g - 1, 0, 512)
+                    multiply(g - 1, 0, 512)
+            if g < 2:
+                interleave(g, 0, 4, 0, 256)
+                interleave(g, 0, 4, 256, 512)
+            if g == 2:
+                interleave(g, 2, 4, 0, 256)
+                interleave(g, 2, 4, 256, 512)
+        interleave(3, 2, 4, 0, 256)
+        interleave(3, 2, 4, 256, 512, vector=True)
         quantize(3, 0, 256)
         multiply(3, 0, 256)
-        interleave(3, 384, 512, vector=True)
-        quantize(3, 256, 384)
-        multiply(3, 256, 384)
-        finish(0, 384)
-        quantize(3, 384, 512)
-        multiply(3, 384, 512)
-        finish(384, 512)
+        quantize(3, 256, 512)
+        multiply(3, 256, 512)
+        finish(0, 256)
+        finish(256, 512)

@@ -49,13 +49,13 @@ def tile_list_heads_silu_kernel(tc, xT, w_words, w_scales, wgt, b, offs, out):
         nc.sync.dma_start(lists[:], offs)
         nc.scalar.dma_start(out=factors[:, 0:256], in_=wgt[:, 0:256])
         load_plane(0)
-        for r in range(4):
-            nc.scalar.dma_start(out=wscales[r:P:32, :, :].bitcast(I32), in_=scale_rows[r])
         nc.scalar.activation(warm[:], warm[:], SILU)
         nc.sync.dma_start(out=factors[:, 256:512], in_=wgt[:, 256:512])
         for u in range(1, 10):
             load_plane(u)
         nc.sync.dma_start(out=words[:].bitcast(I32), in_=w_words.bitcast(I32).rearrange("a p n -> p a n"))
+        for r in range(4):
+            nc.sync.dma_start(out=wscales[r:P:32, :, :].bitcast(I32), in_=scale_rows[r])
         for u in range(10, 16):
             load_plane(u)
         nc.sync.dma_start(out=bias[:], in_=b.rearrange("(c p) -> p c", p=P))
@@ -99,27 +99,39 @@ def tile_list_heads_silu_kernel(tc, xT, w_words, w_scales, wgt, b, offs, out):
                     nc.scalar.activation(result[m][:, BLOCK * j : BLOCK * (j + 1)], sums[m][j][:], SILU, bias=bias[:, m : m + 1])
                 nc.sync.dma_start(out=out[P * m : P * (m + 1), lo:hi], in_=result[m][:, lo:hi])
 
-        for g in range(PASSES):
+        for g in range(3):
             for t in range(PACK):
                 gather(g, t, 0, 256)
                 gather(g, t, 256, 512)
-                if t == 1 and g >= 2:
+                if t == 1 and g == 2:
                     interleave(g, 0, 2, 0, 256)
                     interleave(g, 0, 2, 256, 512)
                 if t == 2 and g >= 1:
                     quantize(g - 1, 0, 512)
                     multiply(g - 1, 0, 512)
-            if g < 2:
-                interleave(g, 0, 4, 0, 256)
-                interleave(g, 0, 4, 256, 512)
-            if g == 2:
-                interleave(g, 2, 4, 0, 256)
-                interleave(g, 2, 4, 256, 512)
+            first = 2 if g == 2 else 0
+            interleave(g, first, 4, 0, 256)
+            interleave(g, first, 4, 256, 512)
+        for t in range(2):
+            gather(3, t, 0, 256)
+            gather(3, t, 256, 512)
+        interleave(3, 0, 2, 0, 256)
+        interleave(3, 0, 2, 256, 512)
+        gather(3, 2, 0, 384)
+        quantize(2, 0, 512)
+        multiply(2, 0, 512)
+        gather(3, 3, 0, 384)
         interleave(3, 2, 4, 0, 256)
-        interleave(3, 2, 4, 256, 512, vector=True)
+        interleave(3, 2, 4, 256, 384)
+        gather(3, 2, 384, 512)
+        gather(3, 3, 384, 512)
+        interleave(3, 2, 4, 384, 512, vector=True)
         quantize(3, 0, 256)
         multiply(3, 0, 256)
-        quantize(3, 256, 512)
-        multiply(3, 256, 512)
+        quantize(3, 384, 512)
+        multiply(3, 384, 512)
+        quantize(3, 256, 384)
+        multiply(3, 256, 384)
         finish(0, 256)
-        finish(256, 512)
+        finish(384, 512)
+        finish(256, 384)

import concourse.mybir as mybir

K, M, T, S = 2048, 256, 1024, 512
FLOPS = 2 * K * M * S

P = 128
PACK = 4
PASSES = K // (P * PACK)
BLOCK = 128

F32 = mybir.dt.float32
BF16 = mybir.dt.bfloat16
I32 = mybir.dt.int32
U32 = mybir.dt.uint32
U16 = mybir.dt.uint16
U8 = mybir.dt.uint8
FP8X4 = mybir.dt.float8_e4m3fn_x4
FP4X4 = mybir.dt.float4_e2m1fn_x4
MULT = mybir.AluOpType.mult
SILU = mybir.ActivationFunctionType.Silu


def tile_list_heads_silu_kernel(tc, xT, w_words, w_scales, wgt, b, offs, out):
    nc = tc.nc
    with tc.tile_pool(name="held", bufs=1) as held, tc.psum_pool(name="psum", bufs=1) as psum:
        lists = held.tile([P, S // 16], U16, name="lists")
        factors = held.tile([P, S], F32, name="factors")
        planes = [held.tile([P, T], F32, name=f"plane{u}") for u in range(PASSES * PACK)]
        words = held.tile([P, PASSES, 2 * M], U8, name="words", align_bytes=64)
        wscales = held.tile([P, PASSES, M], U8, name="wscales", align_bytes=64)
        bias = held.tile([P, 2], F32, name="bias")
        warm = held.tile([P, 1], F32, name="warm")
        picked = [held.tile([P, PACK, S], F32, name=f"picked{g}") for g in range(PASSES)]
        packed = [held.tile([P, S, PACK], BF16, name=f"packed{g}", align_bytes=64) for g in range(PASSES)]
        codes = [held.tile([P, S], U32, name=f"codes{g}", align_bytes=64) for g in range(PASSES)]
        scales = [held.tile([P, S], U8, name=f"scales{g}", align_bytes=64) for g in range(PASSES)]
        result = [held.tile([P, S], F32, name=f"result{m}") for m in range(2)]
        sums = [[psum.tile([P, BLOCK], F32, name=f"sum{m}_{j}") for j in range(S // BLOCK)] for m in range(2)]

        nc.vector.memset(wscales[:].rearrange("p a n -> p (a n)").bitcast(I32), 0)
        nc.vector.memset(warm[:], 0.0)

        x_planes = xT.rearrange("(a p i) t -> a i p t", p=P, i=PACK)
        scale_rows = w_scales.bitcast(I32).rearrange("a (q r) n -> r q a n", r=4)

        def load_plane(u):
            nc.sync.dma_start(out=planes[u][:], in_=x_planes[u // PACK, u % PACK])

        nc.sync.dma_start(lists[:], offs)
        nc.scalar.dma_start(out=factors[:, 0:256], in_=wgt[:, 0:256])
        load_plane(0)
        nc.scalar.activation(warm[:], warm[:], SILU)
        nc.sync.dma_start(out=factors[:, 256:512], in_=wgt[:, 256:512])
        for u in range(1, 10):
            load_plane(u)
        nc.sync.dma_start(out=words[:].bitcast(I32), in_=w_words.bitcast(I32).rearrange("a p n -> p a n"))
        for r in range(4):
            nc.sync.dma_start(out=wscales[r:P:32, :, :].bitcast(I32), in_=scale_rows[r])
        for u in range(10, 16):
            load_plane(u)
        nc.sync.dma_start(out=bias[:], in_=b.rearrange("(c p) -> p c", p=P))

        def gather(g, t, lo, hi):
            nc.vector.tensor_tensor(
                picked[g][:, t, lo:hi], planes[PACK * g + t][:].indirect(lists[:, lo // 16 : hi // 16]), factors[:, lo:hi], MULT
            )

        def interleave(g, t0, t1, lo, hi, vector=False):
            src = picked[g][:, t0:t1, lo:hi].rearrange("p t n -> p n t")
            if vector:
                nc.vector.tensor_copy(packed[g][:, lo:hi, t0:t1], src)
            else:
                nc.scalar.copy(packed[g][:, lo:hi, t0:t1], src)

        def quantize(g, lo, hi):
            nc.vector.quantize_mx(
                out=codes[g][:, lo:hi].bitcast(FP8X4),
                scales=scales[g][:, lo:hi],
                in_=packed[g][:, lo:hi, :].rearrange("p n t -> p (n t)"),
            )

        def multiply(g, lo, hi):
            for j in range(lo // BLOCK, hi // BLOCK):
                cols = slice(BLOCK * j, BLOCK * (j + 1))
                for m in range(2):
                    nc.tensor.matmul_mx(
                        out=sums[m][j][:],
                        lhsT=words[:, g, 256 * m : 256 * (m + 1)].bitcast(FP4X4),
                        lhsT_scale=wscales[:, g, P * m : P * (m + 1)],
                        rhs=codes[g][:, cols].bitcast(FP8X4),
                        rhs_scale=scales[g][:, cols],
                        start=(g == 0),
                        stop=(g == PASSES - 1),
                    )

        def finish(lo, hi):
            for m in range(2):
                for j in range(lo // BLOCK, hi // BLOCK):
                    nc.scalar.activation(result[m][:, BLOCK * j : BLOCK * (j + 1)], sums[m][j][:], SILU, bias=bias[:, m : m + 1])
                nc.sync.dma_start(out=out[P * m : P * (m + 1), lo:hi], in_=result[m][:, lo:hi])

        for g in range(3):
            for t in range(PACK):
                gather(g, t, 0, 256)
                gather(g, t, 256, 512)
                if t == 1 and g == 2:
                    interleave(g, 0, 2, 0, 256)
                    interleave(g, 0, 2, 256, 512)
                if t == 2 and g >= 1:
                    quantize(g - 1, 0, 512)
                    multiply(g - 1, 0, 512)
            first = 2 if g == 2 else 0
            interleave(g, first, 4, 0, 256)
            interleave(g, first, 4, 256, 512)
        for t in range(2):
            gather(3, t, 0, 256)
            gather(3, t, 256, 512)
        interleave(3, 0, 2, 0, 256)
        interleave(3, 0, 2, 256, 512)
        gather(3, 2, 0, 384)
        quantize(2, 0, 512)
        multiply(2, 0, 512)
        gather(3, 3, 0, 384)
        interleave(3, 2, 4, 0, 256)
        interleave(3, 2, 4, 256, 384)
        gather(3, 2, 384, 512)
        gather(3, 3, 384, 512)
        interleave(3, 2, 4, 384, 512, vector=True)
        quantize(3, 0, 256)
        multiply(3, 0, 256)
        quantize(3, 384, 512)
        multiply(3, 384, 512)
        quantize(3, 256, 384)
        multiply(3, 256, 384)
        finish(0, 256)
        finish(384, 512)
        finish(256, 384)
